import numpy as np
import ml_dtypes


def mxq(x, axis, fmt="e4m3"):
    dtype, down = {"e4m3": (ml_dtypes.float8_e4m3fn, 7), "e5m2": (ml_dtypes.float8_e5m2, 14)}[fmt]
    v = np.moveaxis(np.asarray(x, np.float32).astype(ml_dtypes.bfloat16).astype(np.float64), axis, -1)
    blocks = v.reshape(v.shape[:-1] + (-1, 32))
    amax = np.abs(blocks).max(-1, keepdims=True)
    byte = np.maximum(np.where(amax > 0, np.frexp(amax)[1] - 1 + 127, 0) - down, 1)
    scale = np.exp2(byte - 127.0)
    codes = (blocks / scale).astype(np.float32).astype(dtype).astype(np.float64)
    return np.moveaxis((codes * scale).reshape(v.shape), -1, axis)


WIDE = False


def mx_kscale(k):
    if not WIDE:
        return np.ones(k)
    levels = np.array([10, -10, 5, -5, 0])
    if k % 512:
        return np.exp2(np.random.permutation(np.resize(levels, k // 32))).repeat(32)
    a = np.empty((k // 512, 16))
    for p in range(k // 512):
        a[p, :8] = np.random.permutation(np.resize(levels, 8))
        for g in range(8):
            far = levels[np.abs(levels - a[p, g]) >= 10]
            a[p, g + 8] = far[np.random.randint(len(far))]
    return np.exp2(a.ravel()).repeat(32)


def f64(x):
    return np.asarray(x).astype(np.float64)


def striped(idx):
    return np.tile(np.asarray(idx).reshape(-1, 16).T, (8, 1)).astype(np.uint16)


def unstriped(offs):
    return offs[:16].T.reshape(-1).astype(np.int64)


E2M1 = np.array([0.0, 0.5, 1.0, 1.5, 2.0, 3.0, 4.0, 6.0, -0.0, -0.5, -1.0, -1.5, -2.0, -3.0, -4.0, -6.0])


def pack_weight(w, fmt):
    k, n = w.shape
    w = f64(np.asarray(w, np.float32).astype(ml_dtypes.bfloat16)).reshape(k // 32, 32, n)
    amax = np.abs(w).max(1)
    if fmt == "e4m3":
        byte = np.frexp(amax)[1] - 1 + 127 - 7
    else:
        mant, ex = np.frexp(amax / 6.0)
        byte = np.where(mant > 0.5, ex, ex - 1) + 127
    byte = np.clip(np.where(amax > 0, byte, 1), 1, 254)
    scaled = (w * np.exp2(127.0 - byte)[:, None, :]).reshape(k, n).astype(np.float32)
    by_word = np.ascontiguousarray(scaled.reshape(k // 512, 128, 4, n).transpose(0, 1, 3, 2))
    if fmt == "e4m3":
        words = by_word.astype(ml_dtypes.float8_e4m3fn).view(np.uint8)
    else:
        c = by_word.astype(ml_dtypes.float4_e2m1fn).view(np.uint8) & 0xF
        words = (c[..., 0::2] | (c[..., 1::2] << 4)).reshape(k // 512, 128, 2 * n)
    return np.ascontiguousarray(words), np.ascontiguousarray(byte.astype(np.uint8).reshape(k // 512, 16, n))


def unpack_weight(words, scales, fmt):
    g, _, n = scales.shape
    words = np.ascontiguousarray(words).reshape(g, 128, n, -1)
    if fmt == "e4m3":
        vals = words.view(ml_dtypes.float8_e4m3fn).astype(np.float64)
    else:
        nib = np.empty((g, 128, n, 4), np.uint8)
        nib[..., 0::2] = words & 0xF
        nib[..., 1::2] = words >> 4
        vals = E2M1[nib]
    vals = vals * np.repeat(np.exp2(scales.astype(np.float64) - 127.0), 8, axis=1)[..., None]
    return vals.transpose(0, 1, 3, 2).reshape(g * 512, n)


K, T, J, I, R, S, L, N = 1024, 2048, 512, 256, 512, 512, 512, 512


def setup_inputs():
    n = np.random.standard_normal
    idx = np.random.permutation(T)[:J]
    idx2 = np.random.permutation(J)[:I]
    idx3 = np.random.randint(0, I, S)
    fk = mx_kscale(K)
    fr = mx_kscale(R)
    fl = mx_kscale(L)
    xtp = pack_weight(n((K, T)) / fk[:, None], "e4m3")
    wap = pack_weight(n((K, R)) * 1 / np.sqrt(K) * fk[:, None] * fr, "e2m1")
    wbp = pack_weight(n((R, N)) * 1 / np.sqrt(R) / fr[:, None], "e4m3")
    rdp = pack_weight(n((L, S)) / fl[:, None], "e2m1")
    wrp = pack_weight(n((L, N)) * 1 / np.sqrt(L) * fl[:, None], "e4m3")
    return {
        "xt_words": xtp[0],
        "xt_scales": xtp[1],
        "wa_words": wap[0],
        "wa_scales": wap[1],
        "wb_words": wbp[0],
        "wb_scales": wbp[1],
        "rd_words": rdp[0],
        "rd_scales": rdp[1],
        "wr_words": wrp[0],
        "wr_scales": wrp[1],
        "offs": striped(idx),
        "offs2": striped(idx2),
        "offs3": striped(idx3),
    }


def reference(xt_words, xt_scales, wa_words, wa_scales, wb_words, wb_scales, rd_words, rd_scales, wr_words, wr_scales, offs, offs2, offs3):
    idx = unstriped(offs)
    idx2 = unstriped(offs2)
    idx3 = unstriped(offs3)
    xtu = unpack_weight(xt_words, xt_scales, "e4m3")
    wau = unpack_weight(wa_words, wa_scales, "e2m1")
    wbu = unpack_weight(wb_words, wb_scales, "e4m3")
    rdu = unpack_weight(rd_words, rd_scales, "e2m1")
    wru = unpack_weight(wr_words, wr_scales, "e4m3")
    xtidxg = xtu[:, idx]
    a = wau.T @ xtidxg
    hid = np.maximum(a, 0.0)
    hididx2q = mxq(hid[:, idx2], 0, "e4m3")
    p = wbu.T @ hididx2q
    q = wru.T @ rdu
    y = p[:, idx3] * q
    return y

@@ -1,0 +1,153 @@
+from contextlib import ExitStack
+
+import concourse.mybir as mybir
+
+K, T, J, I, R, S, L, N = 1024, 2048, 512, 256, 512, 512, 512, 512
+FLOPS = 2 * (K * R * J + R * N * I + L * N * S)
+
+F32 = mybir.dt.float32
+BF16 = mybir.dt.bfloat16
+I32 = mybir.dt.int32
+U32 = mybir.dt.uint32
+U16 = mybir.dt.uint16
+U8 = mybir.dt.uint8
+E4M3X4 = mybir.dt.float8_e4m3fn_x4
+E2M1X4 = mybir.dt.float4_e2m1fn_x4
+RELU = mybir.ActivationFunctionType.Relu
+MULT = mybir.AluOpType.mult
+
+P = 128
+PACK = 4
+PASSES = K // (P * PACK)
+QUADS = 4
+P_WINDOW = S + 16
+
+
+def load_scale_rows(queue, plane, scales):
+    passes = scales.shape[0]
+    for quad in range(QUADS):
+        queue.dma_start(
+            out=plane[32 * quad : 32 * quad + 4, :].bitcast(I32).rearrange("r (z c) -> r z c", z=passes),
+            in_=scales[:, 4 * quad : 4 * quad + 4, :].bitcast(I32).rearrange("z r c -> r z c"),
+        )
+
+
+def tile_list_three_list_relay_kernel(tc, xt_words, xt_scales, wa_words, wa_scales, wb_words, wb_scales,
+                                           rd_words, rd_scales, wr_words, wr_scales, offs, offs2, offs3, out):
+    nc = tc.nc
+    with ExitStack() as ctx:
+        lists = ctx.enter_context(tc.tile_pool(name="lists", bufs=1))
+        sb = ctx.enter_context(tc.tile_pool(name="sb", bufs=1))
+        psum = ctx.enter_context(tc.psum_pool(name="psum", bufs=1))
+
+        idx = lists.tile([P, J // 16], U16, name="idx")
+        idx2 = lists.tile([P, I // 16], U16, name="idx2")
+        idx3 = lists.tile([P, S // 16], U16, name="idx3")
+
+        xs = sb.tile([P, PASSES * T], U8, name="xs", align_bytes=64)
+        nc.vector.memset(xs[:].bitcast(I32), 0)
+        load_scale_rows(nc.scalar, xs, xt_scales)
+        zeros = sb.tile([P, P_WINDOW - I], F32, name="zeros")
+        nc.vector.memset(zeros[:], 0.0)
+
+        stage_s = sb.tile([P, PASSES * R], U8, name="stage_s", align_bytes=64)
+        nc.gpsimd.memset(stage_s[:].bitcast(I32), 0)
+        load_scale_rows(nc.gpsimd, stage_s, wa_scales)
+        wr_s = sb.tile([P, N], U8, name="wr_s", align_bytes=64)
+        nc.gpsimd.memset(wr_s[:].bitcast(I32), 0)
+        load_scale_rows(nc.gpsimd, wr_s, wr_scales)
+
+        nc.sync.dma_start(idx[:], offs)
+        wa_raw = []
+        for z in range(PASSES):
+            raw = sb.tile([P, R], U16, name=f"wa_raw{z}", tag=f"stage{z}", align_bytes=64)
+            nc.sync.dma_start(out=raw[:].bitcast(I32), in_=wa_words[z].bitcast(I32))
+            wa_raw.append(raw)
+        nc.sync.dma_start(idx2[:], offs2)
+        xw = [sb.tile([P, T], U32, name=f"xw{z}", align_bytes=64) for z in range(PASSES)]
+        nc.sync.dma_start(out=xw[0][:].bitcast(I32), in_=xt_words[0].rearrange("p c r -> p (c r)").bitcast(I32))
+        nc.sync.dma_start(idx3[:], offs3)
+        nc.sync.dma_start(out=xw[1][:].bitcast(I32), in_=xt_words[1].rearrange("p c r -> p (c r)").bitcast(I32))
+        rd_w = sb.tile([P, S], U16, name="rd_w", align_bytes=64)
+        nc.sync.dma_start(out=rd_w[:].bitcast(I32), in_=rd_words[0].bitcast(I32))
+
+        p_win = [sb.tile([P, P_WINDOW], F32, name=f"p_win{c}", align_bytes=64) for c in range(N // P)]
+        for c in range(N // P):
+            nc.scalar.activation(out=p_win[c][:, I:], in_=zeros[:], func=RELU)
+
+        wa_w = [sb.tile([P, R], U16, name=f"wa_w{z}", align_bytes=64) for z in range(PASSES)]
+        for z in range(PASSES):
+            nc.vector.tensor_copy(out=wa_w[z][:].rearrange("p (t m) -> p t m", t=PACK),
+                                  in_=wa_raw[z][:].rearrange("p (m t) -> p t m", t=PACK))
+        wr_w = sb.tile([P, N], U32, name="wr_w", tag="stage0", align_bytes=64)
+        nc.sync.dma_start(out=wr_w[:].bitcast(I32), in_=wr_words[0].rearrange("p c r -> p (c r)").bitcast(I32))
+        wb_w = sb.tile([P, N], U32, name="wb_w", tag="stage1", align_bytes=64)
+        nc.sync.dma_start(out=wb_w[:].bitcast(I32), in_=wb_words[0].rearrange("p c r -> p (c r)").bitcast(I32))
+
+        xg_s = [sb.tile([P, J], U8, name=f"xg_s{z}", align_bytes=64) for z in range(PASSES)]
+        xg_w = [sb.tile([P, J], U32, name=f"xg_w{z}", align_bytes=64) for z in range(PASSES)]
+        for z in range(PASSES):
+            nc.vector.tensor_copy(out=xg_s[z][:], in_=xs[:, z * T : (z + 1) * T].indirect(idx[:]))
+        nc.vector.tensor_copy(out=xg_w[0][:], in_=xw[0][:].indirect(idx[:]))
+        wa_s = sb.tile([P, PASSES * R], U8, name="wa_s", align_bytes=64)
+        nc.vector.tensor_copy(out=wa_s[:].rearrange("p (z t m) -> p z t m", z=PASSES, t=PACK),
+                              in_=stage_s[:].rearrange("p (z m t) -> p z t m", z=PASSES, t=PACK))
+        nc.vector.tensor_copy(out=xg_w[1][:], in_=xw[1][:].indirect(idx[:]))
+
+        rd_s = stage_s[:, 0:S]
+        wb_s = stage_s[:, S : S + N]
+        load_scale_rows(nc.sync, rd_s, rd_scales)
+        load_scale_rows(nc.sync, wb_s, wb_scales)
+
+        a_ps = [psum.tile([P, J], F32, name=f"a_ps{t}", tag=f"bank{t}") for t in range(PACK)]
+        for z in range(PASSES):
+            for t in range(PACK):
+                nc.tensor.matmul_mx(
+                    out=a_ps[t][:],
+                    lhsT=wa_w[z][:, t * P : (t + 1) * P].bitcast(E2M1X4),
+                    lhsT_scale=wa_s[:, z * R + t * P : z * R + (t + 1) * P],
+                    rhs=xg_w[z][:].bitcast(E4M3X4),
+                    rhs_scale=xg_s[z][:],
+                    start=(z == 0), stop=(z == PASSES - 1),
+                )
+        hid = [sb.tile([P, J], F32, name=f"hid{t}", align_bytes=64) for t in range(PACK)]
+        picked = sb.tile([P, PACK * I], BF16, name="picked", align_bytes=64)
+        for t in range(PACK):
+            nc.scalar.activation(out=hid[t][:], in_=a_ps[t][:], func=RELU)
+            nc.vector.tensor_copy(out=picked[:, t * I : (t + 1) * I], in_=hid[t][:].indirect(idx2[:]))
+
+        q_sb = [sb.tile([P, S], F32, name=f"q_sb{c}", align_bytes=64) for c in range(N // P)]
+        for c in range(N // P):
+            q_ps = psum.tile([P, S], F32, name=f"q_ps{c}")
+            nc.tensor.matmul_mx(
+                out=q_ps[:],
+                lhsT=wr_w[:, c * P : (c + 1) * P].bitcast(E4M3X4),
+                lhsT_scale=wr_s[:, c * P : (c + 1) * P],
+                rhs=rd_w[:].bitcast(E2M1X4),
+                rhs_scale=rd_s,
+                start=True, stop=True,
+            )
+            nc.scalar.copy(out=q_sb[c][:], in_=q_ps[:])
+
+        woven = sb.tile([P, I * PACK], BF16, name="woven", align_bytes=64)
+        nc.vector.tensor_copy(out=woven[:].rearrange("p (c i t) -> p c t i", i=4, t=PACK),
+                              in_=picked[:].rearrange("p (t c i) -> p c t i", i=4, t=PACK))
+        h_w = sb.tile([P, I], U32, name="h_w", align_bytes=64)
+        h_s = sb.tile([P, I], U8, name="h_s", align_bytes=64)
+        nc.vector.quantize_mx(out=h_w[:].bitcast(E4M3X4), scales=h_s[:], in_=woven[:])
+
+        for c in range(N // P):
+            p_ps = psum.tile([P, I], F32, name=f"p_ps{c}", tag=f"bank{c}")
+            nc.tensor.matmul_mx(
+                out=p_ps[:],
+                lhsT=wb_w[:, c * P : (c + 1) * P].bitcast(E4M3X4),
+                lhsT_scale=wb_s[:, c * P : (c + 1) * P],
+                rhs=h_w[:].bitcast(E4M3X4),
+                rhs_scale=h_s[:],
+                start=True, stop=True,
+            )
+            nc.scalar.copy(out=p_win[c][:, 0:I], in_=p_ps[:])
+        for c in range(N // P):
+            y = sb.tile([P, S], F32, name=f"y{c}", align_bytes=64)
+            nc.vector.tensor_tensor(out=y[:], in0=p_win[c][:].indirect(idx3[:]), in1=q_sb[c][:], op=MULT)
+            nc.sync.dma_start(out=out[c * P : (c + 1) * P, :], in_=y[:])

@@ -23,10 +23,10 @@ QUADS = 4
 P_WINDOW = S + 16
 
 
-def load_scale_rows(queue, plane, scales):
+def load_scale_rows(queues, plane, scales):
     passes = scales.shape[0]
     for quad in range(QUADS):
-        queue.dma_start(
+        queues[quad].dma_start(
             out=plane[32 * quad : 32 * quad + 4, :].bitcast(I32).rearrange("r (z c) -> r z c", z=passes),
             in_=scales[:, 4 * quad : 4 * quad + 4, :].bitcast(I32).rearrange("z r c -> r z c"),
         )
@@ -44,110 +44,137 @@ def tile_list_three_list_relay_kernel(tc, xt_words, xt_scales, wa_words, wa_scal
         idx2 = lists.tile([P, I // 16], U16, name="idx2")
         idx3 = lists.tile([P, S // 16], U16, name="idx3")
 
-        xs = sb.tile([P, PASSES * T], U8, name="xs", align_bytes=64)
+        wa_raw = sb.tile([P, PASSES * R], U16, name="wa_raw", align_bytes=64)
+        nc.gpsimd.dma_start(out=wa_raw[:].bitcast(I32).rearrange("p (z c) -> p z c", z=PASSES),
+                            in_=wa_words.bitcast(I32).rearrange("z p c -> p z c"))
+
+        xs = sb.tile([P, T], U8, name="xs", tag="xs", align_bytes=64)
         nc.vector.memset(xs[:].bitcast(I32), 0)
-        load_scale_rows(nc.scalar, xs, xt_scales)
-        zeros = sb.tile([P, P_WINDOW - I], F32, name="zeros")
-        nc.vector.memset(zeros[:], 0.0)
-
+        for quad in range(QUADS):
+            nc.sync.dma_start(out=xs[32 * quad : 32 * quad + 8, :].bitcast(I32),
+                              in_=xt_scales[:, 4 * quad : 4 * quad + 4, :].bitcast(I32))
+        zeros = sb.tile([P, PASSES * R // 4], I32, name="zeros", tag="xw", align_bytes=64)
+        nc.vector.memset(zeros[:], 0)
         stage_s = sb.tile([P, PASSES * R], U8, name="stage_s", align_bytes=64)
-        nc.gpsimd.memset(stage_s[:].bitcast(I32), 0)
-        load_scale_rows(nc.gpsimd, stage_s, wa_scales)
-        wr_s = sb.tile([P, N], U8, name="wr_s", align_bytes=64)
-        nc.gpsimd.memset(wr_s[:].bitcast(I32), 0)
-        load_scale_rows(nc.gpsimd, wr_s, wr_scales)
-
-        nc.sync.dma_start(idx[:], offs)
-        wa_raw = []
-        for z in range(PASSES):
-            raw = sb.tile([P, R], U16, name=f"wa_raw{z}", tag=f"stage{z}", align_bytes=64)
-            nc.sync.dma_start(out=raw[:].bitcast(I32), in_=wa_words[z].bitcast(I32))
-            wa_raw.append(raw)
-        nc.sync.dma_start(idx2[:], offs2)
-        xw = [sb.tile([P, T], U32, name=f"xw{z}", align_bytes=64) for z in range(PASSES)]
-        nc.sync.dma_start(out=xw[0][:].bitcast(I32), in_=xt_words[0].rearrange("p c r -> p (c r)").bitcast(I32))
-        nc.sync.dma_start(idx3[:], offs3)
-        nc.sync.dma_start(out=xw[1][:].bitcast(I32), in_=xt_words[1].rearrange("p c r -> p (c r)").bitcast(I32))
-        rd_w = sb.tile([P, S], U16, name="rd_w", align_bytes=64)
-        nc.sync.dma_start(out=rd_w[:].bitcast(I32), in_=rd_words[0].bitcast(I32))
+        nc.vector.tensor_copy(out=stage_s[:].bitcast(I32), in_=zeros[:])
+        xg_s = [sb.tile([P, J], U8, name=f"xg_s{z}", align_bytes=64) for z in range(PASSES)]
+        nc.vector.memset(xg_s[1][:].bitcast(I32), 0)
 
         p_win = [sb.tile([P, P_WINDOW], F32, name=f"p_win{c}", align_bytes=64) for c in range(N // P)]
-        for c in range(N // P):
-            nc.scalar.activation(out=p_win[c][:, I:], in_=zeros[:], func=RELU)
+        nc.gpsimd.memset(p_win[0][:, I:], 0.0)
+        for c in range(1, N // P):
+            nc.scalar.activation(out=p_win[c][:, I:], in_=p_win[0][:, I:], func=RELU)
+        wr_s = sb.tile([P, N], U8, name="wr_s", align_bytes=64)
+        nc.gpsimd.memset(wr_s[:].bitcast(I32), 0)
+        load_scale_rows([nc.gpsimd] * QUADS, wr_s, wr_scales)
 
-        wa_w = [sb.tile([P, R], U16, name=f"wa_w{z}", align_bytes=64) for z in range(PASSES)]
-        for z in range(PASSES):
-            nc.vector.tensor_copy(out=wa_w[z][:].rearrange("p (t m) -> p t m", t=PACK),
-                                  in_=wa_raw[z][:].rearrange("p (m t) -> p t m", t=PACK))
-        wr_w = sb.tile([P, N], U32, name="wr_w", tag="stage0", align_bytes=64)
-        nc.sync.dma_start(out=wr_w[:].bitcast(I32), in_=wr_words[0].rearrange("p c r -> p (c r)").bitcast(I32))
-        wb_w = sb.tile([P, N], U32, name="wb_w", tag="stage1", align_bytes=64)
-        nc.sync.dma_start(out=wb_w[:].bitcast(I32), in_=wb_words[0].rearrange("p c r -> p (c r)").bitcast(I32))
+        nc.sync.dma_start(idx[:], offs)
+        xw = sb.tile([P, PASSES * T], U32, name="xw", tag="xw", align_bytes=64)
+        nc.sync.dma_start(out=xw[:, 0:T].bitcast(I32), in_=xt_words[0].rearrange("p c r -> p (c r)").bitcast(I32))
+        load_scale_rows([nc.sync] * QUADS, stage_s, wa_scales)
+        nc.sync.dma_start(out=xw[:, T:].bitcast(I32), in_=xt_words[1].rearrange("p c r -> p (c r)").bitcast(I32))
+        nc.sync.dma_start(idx2[:], offs2)
+        nc.sync.dma_start(idx3[:], offs3)
 
-        xg_s = [sb.tile([P, J], U8, name=f"xg_s{z}", align_bytes=64) for z in range(PASSES)]
         xg_w = [sb.tile([P, J], U32, name=f"xg_w{z}", align_bytes=64) for z in range(PASSES)]
-        for z in range(PASSES):
-            nc.vector.tensor_copy(out=xg_s[z][:], in_=xs[:, z * T : (z + 1) * T].indirect(idx[:]))
-        nc.vector.tensor_copy(out=xg_w[0][:], in_=xw[0][:].indirect(idx[:]))
+        nc.vector.tensor_copy(out=xg_s[0][:], in_=xs[:].indirect(idx[:]))
+        for quad in range(QUADS):
+            nc.sync.dma_start(out=xg_s[1][32 * quad : 32 * quad + 4, :].bitcast(I32),
+                              in_=xg_s[0][32 * quad + 4 : 32 * quad + 8, :].bitcast(I32))
+        wa_w = sb.tile([P, PASSES * R], U16, name="wa_w", align_bytes=64)
+        nc.vector.tensor_copy(out=wa_w[:].rearrange("p (z t b i) -> p z b t i", z=PASSES, t=PACK, i=8),
+                              in_=wa_raw[:].rearrange("p (z b i t) -> p z b t i", z=PASSES, t=PACK, i=8))
+        nc.vector.tensor_copy(out=xg_w[0][:], in_=xw[:, 0:T].indirect(idx[:]))
         wa_s = sb.tile([P, PASSES * R], U8, name="wa_s", align_bytes=64)
-        nc.vector.tensor_copy(out=wa_s[:].rearrange("p (z t m) -> p z t m", z=PASSES, t=PACK),
-                              in_=stage_s[:].rearrange("p (z m t) -> p z t m", z=PASSES, t=PACK))
-        nc.vector.tensor_copy(out=xg_w[1][:], in_=xw[1][:].indirect(idx[:]))
+        for z in range(PASSES):
+            nc.vector.tensor_copy(out=wa_s[:, z * R : (z + 1) * R].rearrange("p (t b i) -> p b t i", t=PACK, i=16),
+                                  in_=stage_s[:, z * R : (z + 1) * R].rearrange("p (b i t) -> p b t i", t=PACK, i=16))
+        for h in range(2):
+            nc.vector.tensor_copy(out=xg_w[1][:, h * J // 2 : (h + 1) * J // 2],
+                                  in_=xw[:, T:].indirect(idx[:, h * J // 32 : (h + 1) * J // 32]))
 
+        late = sb.tile([P, 2 * N + S // 2], U32, name="late", tag="xs", align_bytes=64)
+        wb_w = late[:, 0:N]
+        wr_w = late[:, N : 2 * N]
+        rd_w = late[:, 2 * N :]
+        nc.sync.dma_start(out=wr_w.bitcast(I32), in_=wr_words[0].rearrange("p c r -> p (c r)").bitcast(I32))
+        nc.sync.dma_start(out=rd_w.bitcast(I32), in_=rd_words[0].bitcast(I32))
+        nc.sync.dma_start(out=wb_w.bitcast(I32), in_=wb_words[0].rearrange("p c r -> p (c r)").bitcast(I32))
         rd_s = stage_s[:, 0:S]
         wb_s = stage_s[:, S : S + N]
-        load_scale_rows(nc.sync, rd_s, rd_scales)
-        load_scale_rows(nc.sync, wb_s, wb_scales)
+        load_scale_rows([nc.sync] * QUADS, rd_s, rd_scales)
+        load_scale_rows([nc.sync] * QUADS, wb_s, wb_scales)
 
-        a_ps = [psum.tile([P, J], F32, name=f"a_ps{t}", tag=f"bank{t}") for t in range(PACK)]
-        for z in range(PASSES):
-            for t in range(PACK):
-                nc.tensor.matmul_mx(
-                    out=a_ps[t][:],
-                    lhsT=wa_w[z][:, t * P : (t + 1) * P].bitcast(E2M1X4),
-                    lhsT_scale=wa_s[:, z * R + t * P : z * R + (t + 1) * P],
-                    rhs=xg_w[z][:].bitcast(E4M3X4),
-                    rhs_scale=xg_s[z][:],
-                    start=(z == 0), stop=(z == PASSES - 1),
-                )
+        def first_layer(acc, t, z, col0, width, acc0, start, stop):
+            nc.tensor.matmul_mx(
+                out=acc[:, acc0 : acc0 + width],
+                lhsT=wa_w[:, z * R + t * P : z * R + (t + 1) * P].bitcast(E2M1X4),
+                lhsT_scale=wa_s[:, z * R + t * P : z * R + (t + 1) * P],
+                rhs=xg_w[z][:, col0 : col0 + width].bitcast(E4M3X4),
+                rhs_scale=xg_s[z][:, col0 : col0 + width],
+                start=start, stop=stop,
+            )
+
         hid = [sb.tile([P, J], F32, name=f"hid{t}", align_bytes=64) for t in range(PACK)]
         picked = sb.tile([P, PACK * I], BF16, name="picked", align_bytes=64)
-        for t in range(PACK):
-            nc.scalar.activation(out=hid[t][:], in_=a_ps[t][:], func=RELU)
+        for h in range(2):
+            acc = psum.tile([P, J // 2], F32, name=f"a_half{h}", tag=f"bank{h}")
+            for z in range(PASSES):
+                for u in range(2):
+                    first_layer(acc, 0, z, h * J // 2 + u * P, P, u * P, z == 0 and u == 0, z == PASSES - 1 and u == 1)
+            nc.scalar.activation(out=hid[0][:, h * J // 2 : (h + 1) * J // 2], in_=acc[:], func=RELU)
+        nc.vector.tensor_copy(out=picked[:, 0:I], in_=hid[0][:].indirect(idx2[:]))
+        for t in range(1, PACK):
+            acc = psum.tile([P, J], F32, name=f"a_ps{t}", tag=f"bank{t + 1}")
+            for z in range(PASSES):
+                first_layer(acc, t, z, 0, J, 0, z == 0, z == PASSES - 1)
+            nc.scalar.activation(out=hid[t][:], in_=acc[:], func=RELU)
             nc.vector.tensor_copy(out=picked[:, t * I : (t + 1) * I], in_=hid[t][:].indirect(idx2[:]))
 
-        q_sb = [sb.tile([P, S], F32, name=f"q_sb{c}", align_bytes=64) for c in range(N // P)]
+        woven = sb.tile([P, I * PACK], BF16, name="woven", align_bytes=64)
+        h_w = sb.tile([P, I], U32, name="h_w", align_bytes=64)
+        h_s = sb.tile([P, I], U8, name="h_s", align_bytes=64)
+        for h in range(2):
+            nc.vector.tensor_copy(
+                out=woven[:, h * P * PACK : (h + 1) * P * PACK].rearrange("p (c i t) -> p c t i", i=4, t=PACK),
+                in_=picked[:].rearrange("p (t c i) -> p c t i", i=4, t=PACK)[:, h * P // 4 : (h + 1) * P // 4])
+        for h in range(2):
+            nc.vector.quantize_mx(out=h_w[:, h * P : (h + 1) * P].bitcast(E4M3X4), scales=h_s[:, h * P : (h + 1) * P],
+                                  in_=woven[:, h * P * PACK : (h + 1) * P * PACK])
+
+        def second_layer(c, col0, width, bank):
+            acc = psum.tile([P, width], F32, name=f"p_ps{c}_{col0}", tag=f"bank{bank}")
+            nc.tensor.matmul_mx(
+                out=acc[:],
+                lhsT=wb_w[:, c * P : (c + 1) * P].bitcast(E4M3X4),
+                lhsT_scale=wb_s[:, c * P : (c + 1) * P],
+                rhs=h_w[:, col0 : col0 + width].bitcast(E4M3X4),
+                rhs_scale=h_s[:, col0 : col0 + width],
+                start=True, stop=True,
+            )
+            nc.scalar.copy(out=p_win[c][:, col0 : col0 + width], in_=acc[:])
+
         for c in range(N // P):
-            q_ps = psum.tile([P, S], F32, name=f"q_ps{c}")
+            q_ps = psum.tile([P, S], F32, name=f"q_ps{c}", tag=f"bank{5 + c % 3}")
             nc.tensor.matmul_mx(
                 out=q_ps[:],
                 lhsT=wr_w[:, c * P : (c + 1) * P].bitcast(E4M3X4),
                 lhsT_scale=wr_s[:, c * P : (c + 1) * P],
-                rhs=rd_w[:].bitcast(E2M1X4),
+                rhs=rd_w.bitcast(E2M1X4),
                 rhs_scale=rd_s,
                 start=True, stop=True,
             )
-            nc.scalar.copy(out=q_sb[c][:], in_=q_ps[:])
-
-        woven = sb.tile([P, I * PACK], BF16, name="woven", align_bytes=64)
-        nc.vector.tensor_copy(out=woven[:].rearrange("p (c i t) -> p c t i", i=4, t=PACK),
-                              in_=picked[:].rearrange("p (t c i) -> p c t i", i=4, t=PACK))
-        h_w = sb.tile([P, I], U32, name="h_w", align_bytes=64)
-        h_s = sb.tile([P, I], U8, name="h_s", align_bytes=64)
-        nc.vector.quantize_mx(out=h_w[:].bitcast(E4M3X4), scales=h_s[:], in_=woven[:])
-
-        for c in range(N // P):
-            p_ps = psum.tile([P, I], F32, name=f"p_ps{c}", tag=f"bank{c}")
-            nc.tensor.matmul_mx(
-                out=p_ps[:],
-                lhsT=wb_w[:, c * P : (c + 1) * P].bitcast(E4M3X4),
-                lhsT_scale=wb_s[:, c * P : (c + 1) * P],
-                rhs=h_w[:].bitcast(E4M3X4),
-                rhs_scale=h_s[:],
-                start=True, stop=True,
-            )
-            nc.scalar.copy(out=p_win[c][:, 0:I], in_=p_ps[:])
-        for c in range(N // P):
-            y = sb.tile([P, S], F32, name=f"y{c}", align_bytes=64)
-            nc.vector.tensor_tensor(out=y[:], in0=p_win[c][:].indirect(idx3[:]), in1=q_sb[c][:], op=MULT)
-            nc.sync.dma_start(out=out[c * P : (c + 1) * P, :], in_=y[:])
+            q_sb = sb.tile([P, S], F32, name=f"q_sb{c}", align_bytes=64)
+            nc.scalar.copy(out=q_sb[:], in_=q_ps[:])
+            if c == 0:
+                for h in range(2):
+                    second_layer(c, h * P, P, h)
+            else:
+                second_layer(c, 0, I, c + 1)
+            parts = 2 if c == N // P - 1 else 1
+            for h in range(parts):
+                w = S // parts
+                y = sb.tile([P, w], F32, name=f"y{c}_{h}", align_bytes=64)
+                nc.vector.tensor_tensor(out=y[:], in0=p_win[c][:].indirect(idx3[:, h * w // 16 : (h + 1) * w // 16]),
+                                        in1=q_sb[:, h * w : (h + 1) * w], op=MULT)
+                nc.sync.dma_start(out=out[c * P : (c + 1) * P, h * w : (h + 1) * w], in_=y[:])

@@ -48,13 +48,13 @@ def tile_list_three_list_relay_kernel(tc, xt_words, xt_scales, wa_words, wa_scal
         nc.gpsimd.dma_start(out=wa_raw[:].bitcast(I32).rearrange("p (z c) -> p z c", z=PASSES),
                             in_=wa_words.bitcast(I32).rearrange("z p c -> p z c"))
 
-        xs = sb.tile([P, T], U8, name="xs", tag="xs", align_bytes=64)
-        nc.vector.memset(xs[:].bitcast(I32), 0)
-        for quad in range(QUADS):
-            nc.sync.dma_start(out=xs[32 * quad : 32 * quad + 8, :].bitcast(I32),
-                              in_=xt_scales[:, 4 * quad : 4 * quad + 4, :].bitcast(I32))
         zeros = sb.tile([P, PASSES * R // 4], I32, name="zeros", tag="xw", align_bytes=64)
         nc.vector.memset(zeros[:], 0)
+        xs = sb.tile([P, T], U8, name="xs", tag="xs", align_bytes=64)
+        nc.vector.memset(xs[:].bitcast(I32), 0)
+        for row in range(4):
+            nc.sync.dma_start(out=xs[row:P:16, :].bitcast(I32),
+                              in_=xt_scales.bitcast(I32).rearrange("z (q r) c -> r q z c", r=4)[row])
         stage_s = sb.tile([P, PASSES * R], U8, name="stage_s", align_bytes=64)
         nc.vector.tensor_copy(out=stage_s[:].bitcast(I32), in_=zeros[:])
         xg_s = [sb.tile([P, J], U8, name=f"xg_s{z}", align_bytes=64) for z in range(PASSES)]
@@ -80,7 +80,7 @@ def tile_list_three_list_relay_kernel(tc, xt_words, xt_scales, wa_words, wa_scal
         nc.vector.tensor_copy(out=xg_s[0][:], in_=xs[:].indirect(idx[:]))
         for quad in range(QUADS):
             nc.sync.dma_start(out=xg_s[1][32 * quad : 32 * quad + 4, :].bitcast(I32),
-                              in_=xg_s[0][32 * quad + 4 : 32 * quad + 8, :].bitcast(I32))
+                              in_=xg_s[0][32 * quad + 16 : 32 * quad + 20, :].bitcast(I32))
         wa_w = sb.tile([P, PASSES * R], U16, name="wa_w", align_bytes=64)
         nc.vector.tensor_copy(out=wa_w[:].rearrange("p (z t b i) -> p z b t i", z=PASSES, t=PACK, i=8),
                               in_=wa_raw[:].rearrange("p (z b i t) -> p z b t i", z=PASSES, t=PACK, i=8))
@@ -125,7 +125,7 @@ def tile_list_three_list_relay_kernel(tc, xt_words, xt_scales, wa_words, wa_scal
             nc.scalar.activation(out=hid[0][:, h * J // 2 : (h + 1) * J // 2], in_=acc[:], func=RELU)
         nc.vector.tensor_copy(out=picked[:, 0:I], in_=hid[0][:].indirect(idx2[:]))
         for t in range(1, PACK):
-            acc = psum.tile([P, J], F32, name=f"a_ps{t}", tag=f"bank{t + 1}")
+            acc = psum.tile([P, J], F32, name=f"a_ps{t}", tag=f"bank{(t + 1) % 3}")
             for z in range(PASSES):
                 first_layer(acc, t, z, 0, J, 0, z == 0, z == PASSES - 1)
             nc.scalar.activation(out=hid[t][:], in_=acc[:], func=RELU)
@@ -155,7 +155,7 @@ def tile_list_three_list_relay_kernel(tc, xt_words, xt_scales, wa_words, wa_scal
             nc.scalar.copy(out=p_win[c][:, col0 : col0 + width], in_=acc[:])
 
         for c in range(N // P):
-            q_ps = psum.tile([P, S], F32, name=f"q_ps{c}", tag=f"bank{5 + c % 3}")
+            q_ps = psum.tile([P, S], F32, name=f"q_ps{c}", tag=f"bank{4 + c}")
             nc.tensor.matmul_mx(
                 out=q_ps[:],
                 lhsT=wr_w[:, c * P : (c + 1) * P].bitcast(E4M3X4),
@@ -170,11 +170,10 @@ def tile_list_three_list_relay_kernel(tc, xt_words, xt_scales, wa_words, wa_scal
                 for h in range(2):
                     second_layer(c, h * P, P, h)
             else:
-                second_layer(c, 0, I, c + 1)
-            parts = 2 if c == N // P - 1 else 1
-            for h in range(parts):
-                w = S // parts
-                y = sb.tile([P, w], F32, name=f"y{c}_{h}", align_bytes=64)
-                nc.vector.tensor_tensor(out=y[:], in0=p_win[c][:].indirect(idx3[:, h * w // 16 : (h + 1) * w // 16]),
-                                        in1=q_sb[:, h * w : (h + 1) * w], op=MULT)
-                nc.sync.dma_start(out=out[c * P : (c + 1) * P, h * w : (h + 1) * w], in_=y[:])
+                second_layer(c, 0, I, (c + 1) % 4)
+            cuts = [0, S - P, S] if c == N // P - 1 else [0, S]
+            for s0, s1 in zip(cuts, cuts[1:]):
+                y = sb.tile([P, s1 - s0], F32, name=f"y{c}_{s0}", align_bytes=64)
+                nc.vector.tensor_tensor(out=y[:], in0=p_win[c][:].indirect(idx3[:, s0 // 16 : s1 // 16]),
+                                        in1=q_sb[:, s0:s1], op=MULT)
+                nc.sync.dma_start(out=out[c * P : (c + 1) * P, s0:s1], in_=y[:])

from contextlib import ExitStack

import concourse.mybir as mybir

K, T, J, I, R, S, L, N = 1024, 2048, 512, 256, 512, 512, 512, 512
FLOPS = 2 * (K * R * J + R * N * I + L * N * S)

F32 = mybir.dt.float32
BF16 = mybir.dt.bfloat16
I32 = mybir.dt.int32
U32 = mybir.dt.uint32
U16 = mybir.dt.uint16
U8 = mybir.dt.uint8
E4M3X4 = mybir.dt.float8_e4m3fn_x4
E2M1X4 = mybir.dt.float4_e2m1fn_x4
RELU = mybir.ActivationFunctionType.Relu
MULT = mybir.AluOpType.mult

P = 128
PACK = 4
PASSES = K // (P * PACK)
QUADS = 4
P_WINDOW = S + 16


def load_scale_rows(queues, plane, scales):
    passes = scales.shape[0]
    for quad in range(QUADS):
        queues[quad].dma_start(
            out=plane[32 * quad : 32 * quad + 4, :].bitcast(I32).rearrange("r (z c) -> r z c", z=passes),
            in_=scales[:, 4 * quad : 4 * quad + 4, :].bitcast(I32).rearrange("z r c -> r z c"),
        )


def tile_list_three_list_relay_kernel(tc, xt_words, xt_scales, wa_words, wa_scales, wb_words, wb_scales,
                                           rd_words, rd_scales, wr_words, wr_scales, offs, offs2, offs3, out):
    nc = tc.nc
    with ExitStack() as ctx:
        lists = ctx.enter_context(tc.tile_pool(name="lists", bufs=1))
        sb = ctx.enter_context(tc.tile_pool(name="sb", bufs=1))
        psum = ctx.enter_context(tc.psum_pool(name="psum", bufs=1))

        idx = lists.tile([P, J // 16], U16, name="idx")
        idx2 = lists.tile([P, I // 16], U16, name="idx2")
        idx3 = lists.tile([P, S // 16], U16, name="idx3")

        wa_raw = sb.tile([P, PASSES * R], U16, name="wa_raw", align_bytes=64)
        nc.gpsimd.dma_start(out=wa_raw[:].bitcast(I32).rearrange("p (z c) -> p z c", z=PASSES),
                            in_=wa_words.bitcast(I32).rearrange("z p c -> p z c"))

        zeros = sb.tile([P, PASSES * R // 4], I32, name="zeros", tag="xw", align_bytes=64)
        nc.vector.memset(zeros[:], 0)
        xs = sb.tile([P, T], U8, name="xs", tag="xs", align_bytes=64)
        nc.vector.memset(xs[:].bitcast(I32), 0)
        for row in range(4):
            nc.sync.dma_start(out=xs[row:P:16, :].bitcast(I32),
                              in_=xt_scales.bitcast(I32).rearrange("z (q r) c -> r q z c", r=4)[row])
        stage_s = sb.tile([P, PASSES * R], U8, name="stage_s", align_bytes=64)
        nc.vector.tensor_copy(out=stage_s[:].bitcast(I32), in_=zeros[:])
        xg_s = [sb.tile([P, J], U8, name=f"xg_s{z}", align_bytes=64) for z in range(PASSES)]
        nc.vector.memset(xg_s[1][:].bitcast(I32), 0)

        p_win = [sb.tile([P, P_WINDOW], F32, name=f"p_win{c}", align_bytes=64) for c in range(N // P)]
        nc.gpsimd.memset(p_win[0][:, I:], 0.0)
        for c in range(1, N // P):
            nc.scalar.activation(out=p_win[c][:, I:], in_=p_win[0][:, I:], func=RELU)
        wr_s = sb.tile([P, N], U8, name="wr_s", align_bytes=64)
        nc.gpsimd.memset(wr_s[:].bitcast(I32), 0)
        load_scale_rows([nc.gpsimd] * QUADS, wr_s, wr_scales)

        nc.sync.dma_start(idx[:], offs)
        xw = sb.tile([P, PASSES * T], U32, name="xw", tag="xw", align_bytes=64)
        nc.sync.dma_start(out=xw[:, 0:T].bitcast(I32), in_=xt_words[0].rearrange("p c r -> p (c r)").bitcast(I32))
        load_scale_rows([nc.sync] * QUADS, stage_s, wa_scales)
        nc.sync.dma_start(out=xw[:, T:].bitcast(I32), in_=xt_words[1].rearrange("p c r -> p (c r)").bitcast(I32))
        nc.sync.dma_start(idx2[:], offs2)
        nc.sync.dma_start(idx3[:], offs3)

        xg_w = [sb.tile([P, J], U32, name=f"xg_w{z}", align_bytes=64) for z in range(PASSES)]
        nc.vector.tensor_copy(out=xg_s[0][:], in_=xs[:].indirect(idx[:]))
        for quad in range(QUADS):
            nc.sync.dma_start(out=xg_s[1][32 * quad : 32 * quad + 4, :].bitcast(I32),
                              in_=xg_s[0][32 * quad + 16 : 32 * quad + 20, :].bitcast(I32))
        wa_w = sb.tile([P, PASSES * R], U16, name="wa_w", align_bytes=64)
        nc.vector.tensor_copy(out=wa_w[:].rearrange("p (z t b i) -> p z b t i", z=PASSES, t=PACK, i=8),
                              in_=wa_raw[:].rearrange("p (z b i t) -> p z b t i", z=PASSES, t=PACK, i=8))
        nc.vector.tensor_copy(out=xg_w[0][:], in_=xw[:, 0:T].indirect(idx[:]))
        wa_s = sb.tile([P, PASSES * R], U8, name="wa_s", align_bytes=64)
        for z in range(PASSES):
            nc.vector.tensor_copy(out=wa_s[:, z * R : (z + 1) * R].rearrange("p (t b i) -> p b t i", t=PACK, i=16),
                                  in_=stage_s[:, z * R : (z + 1) * R].rearrange("p (b i t) -> p b t i", t=PACK, i=16))
        for h in range(2):
            nc.vector.tensor_copy(out=xg_w[1][:, h * J // 2 : (h + 1) * J // 2],
                                  in_=xw[:, T:].indirect(idx[:, h * J // 32 : (h + 1) * J // 32]))

        late = sb.tile([P, 2 * N + S // 2], U32, name="late", tag="xs", align_bytes=64)
        wb_w = late[:, 0:N]
        wr_w = late[:, N : 2 * N]
        rd_w = late[:, 2 * N :]
        nc.sync.dma_start(out=wr_w.bitcast(I32), in_=wr_words[0].rearrange("p c r -> p (c r)").bitcast(I32))
        nc.sync.dma_start(out=rd_w.bitcast(I32), in_=rd_words[0].bitcast(I32))
        nc.sync.dma_start(out=wb_w.bitcast(I32), in_=wb_words[0].rearrange("p c r -> p (c r)").bitcast(I32))
        rd_s = stage_s[:, 0:S]
        wb_s = stage_s[:, S : S + N]
        load_scale_rows([nc.sync] * QUADS, rd_s, rd_scales)
        load_scale_rows([nc.sync] * QUADS, wb_s, wb_scales)

        def first_layer(acc, t, z, col0, width, acc0, start, stop):
            nc.tensor.matmul_mx(
                out=acc[:, acc0 : acc0 + width],
                lhsT=wa_w[:, z * R + t * P : z * R + (t + 1) * P].bitcast(E2M1X4),
                lhsT_scale=wa_s[:, z * R + t * P : z * R + (t + 1) * P],
                rhs=xg_w[z][:, col0 : col0 + width].bitcast(E4M3X4),
                rhs_scale=xg_s[z][:, col0 : col0 + width],
                start=start, stop=stop,
            )

        hid = [sb.tile([P, J], F32, name=f"hid{t}", align_bytes=64) for t in range(PACK)]
        picked = sb.tile([P, PACK * I], BF16, name="picked", align_bytes=64)
        for h in range(2):
            acc = psum.tile([P, J // 2], F32, name=f"a_half{h}", tag=f"bank{h}")
            for z in range(PASSES):
                for u in range(2):
                    first_layer(acc, 0, z, h * J // 2 + u * P, P, u * P, z == 0 and u == 0, z == PASSES - 1 and u == 1)
            nc.scalar.activation(out=hid[0][:, h * J // 2 : (h + 1) * J // 2], in_=acc[:], func=RELU)
        nc.vector.tensor_copy(out=picked[:, 0:I], in_=hid[0][:].indirect(idx2[:]))
        for t in range(1, PACK):
            acc = psum.tile([P, J], F32, name=f"a_ps{t}", tag=f"bank{(t + 1) % 3}")
            for z in range(PASSES):
                first_layer(acc, t, z, 0, J, 0, z == 0, z == PASSES - 1)
            nc.scalar.activation(out=hid[t][:], in_=acc[:], func=RELU)
            nc.vector.tensor_copy(out=picked[:, t * I : (t + 1) * I], in_=hid[t][:].indirect(idx2[:]))

        woven = sb.tile([P, I * PACK], BF16, name="woven", align_bytes=64)
        h_w = sb.tile([P, I], U32, name="h_w", align_bytes=64)
        h_s = sb.tile([P, I], U8, name="h_s", align_bytes=64)
        for h in range(2):
            nc.vector.tensor_copy(
                out=woven[:, h * P * PACK : (h + 1) * P * PACK].rearrange("p (c i t) -> p c t i", i=4, t=PACK),
                in_=picked[:].rearrange("p (t c i) -> p c t i", i=4, t=PACK)[:, h * P // 4 : (h + 1) * P // 4])
        for h in range(2):
            nc.vector.quantize_mx(out=h_w[:, h * P : (h + 1) * P].bitcast(E4M3X4), scales=h_s[:, h * P : (h + 1) * P],
                                  in_=woven[:, h * P * PACK : (h + 1) * P * PACK])

        def second_layer(c, col0, width, bank):
            acc = psum.tile([P, width], F32, name=f"p_ps{c}_{col0}", tag=f"bank{bank}")
            nc.tensor.matmul_mx(
                out=acc[:],
                lhsT=wb_w[:, c * P : (c + 1) * P].bitcast(E4M3X4),
                lhsT_scale=wb_s[:, c * P : (c + 1) * P],
                rhs=h_w[:, col0 : col0 + width].bitcast(E4M3X4),
                rhs_scale=h_s[:, col0 : col0 + width],
                start=True, stop=True,
            )
            nc.scalar.copy(out=p_win[c][:, col0 : col0 + width], in_=acc[:])

        for c in range(N // P):
            q_ps = psum.tile([P, S], F32, name=f"q_ps{c}", tag=f"bank{4 + c}")
            nc.tensor.matmul_mx(
                out=q_ps[:],
                lhsT=wr_w[:, c * P : (c + 1) * P].bitcast(E4M3X4),
                lhsT_scale=wr_s[:, c * P : (c + 1) * P],
                rhs=rd_w.bitcast(E2M1X4),
                rhs_scale=rd_s,
                start=True, stop=True,
            )
            q_sb = sb.tile([P, S], F32, name=f"q_sb{c}", align_bytes=64)
            nc.scalar.copy(out=q_sb[:], in_=q_ps[:])
            if c == 0:
                for h in range(2):
                    second_layer(c, h * P, P, h)
            else:
                second_layer(c, 0, I, (c + 1) % 4)
            cuts = [0, S - P, S] if c == N // P - 1 else [0, S]
            for s0, s1 in zip(cuts, cuts[1:]):
                y = sb.tile([P, s1 - s0], F32, name=f"y{c}_{s0}", align_bytes=64)
                nc.vector.tensor_tensor(out=y[:], in0=p_win[c][:].indirect(idx3[:, s0 // 16 : s1 // 16]),
                                        in1=q_sb[:, s0:s1], op=MULT)
                nc.sync.dma_start(out=out[c * P : (c + 1) * P, s0:s1], in_=y[:])
